import numpy as np
import ml_dtypes


def mxq(x, axis, fmt="e4m3"):
    dtype, down = {"e4m3": (ml_dtypes.float8_e4m3fn, 7), "e5m2": (ml_dtypes.float8_e5m2, 14)}[fmt]
    v = np.moveaxis(np.asarray(x, np.float32).astype(ml_dtypes.bfloat16).astype(np.float64), axis, -1)
    blocks = v.reshape(v.shape[:-1] + (-1, 32))
    amax = np.abs(blocks).max(-1, keepdims=True)
    byte = np.maximum(np.where(amax > 0, np.frexp(amax)[1] - 1 + 127, 0) - down, 1)
    scale = np.exp2(byte - 127.0)
    codes = (blocks / scale).astype(np.float32).astype(dtype).astype(np.float64)
    return np.moveaxis((codes * scale).reshape(v.shape), -1, axis)


WIDE = False


def mx_kscale(k):
    if not WIDE:
        return np.ones(k)
    levels = np.array([10, -10, 5, -5, 0])
    if k % 512:
        return np.exp2(np.random.permutation(np.resize(levels, k // 32))).repeat(32)
    a = np.empty((k // 512, 16))
    for p in range(k // 512):
        a[p, :8] = np.random.permutation(np.resize(levels, 8))
        for g in range(8):
            far = levels[np.abs(levels - a[p, g]) >= 10]
            a[p, g + 8] = far[np.random.randint(len(far))]
    return np.exp2(a.ravel()).repeat(32)


def f64(x):
    return np.asarray(x).astype(np.float64)


def striped(idx):
    return np.tile(idx.reshape(-1, 16).T, (8, 1)).astype(np.uint16)


def unstriped(offs):
    return offs[:16].T.reshape(-1).astype(np.int64)


E2M1 = np.array([0.0, 0.5, 1.0, 1.5, 2.0, 3.0, 4.0, 6.0, -0.0, -0.5, -1.0, -1.5, -2.0, -3.0, -4.0, -6.0])


def pack_weight(w, fmt):
    k, n = w.shape
    w = f64(np.asarray(w, np.float32).astype(ml_dtypes.bfloat16)).reshape(k // 32, 32, n)
    amax = np.abs(w).max(1)
    if fmt == "e4m3":
        byte = np.frexp(amax)[1] - 1 + 127 - 7
    else:
        mant, ex = np.frexp(amax / 6.0)
        byte = np.where(mant > 0.5, ex, ex - 1) + 127
    byte = np.clip(np.where(amax > 0, byte, 1), 1, 254)
    scaled = (w * np.exp2(127.0 - byte)[:, None, :]).reshape(k, n).astype(np.float32)
    by_word = np.ascontiguousarray(scaled.reshape(k // 512, 128, 4, n).transpose(0, 1, 3, 2))
    if fmt == "e4m3":
        words = by_word.astype(ml_dtypes.float8_e4m3fn).view(np.uint8)
    else:
        c = by_word.astype(ml_dtypes.float4_e2m1fn).view(np.uint8) & 0xF
        words = (c[..., 0::2] | (c[..., 1::2] << 4)).reshape(k // 512, 128, 2 * n)
    return np.ascontiguousarray(words), np.ascontiguousarray(byte.astype(np.uint8).reshape(k // 512, 16, n))


def unpack_weight(words, scales, fmt):
    g, _, n = scales.shape
    words = np.ascontiguousarray(words).reshape(g, 128, n, -1)
    if fmt == "e4m3":
        vals = words.view(ml_dtypes.float8_e4m3fn).astype(np.float64)
    else:
        nib = np.empty((g, 128, n, 4), np.uint8)
        nib[..., 0::2] = words & 0xF
        nib[..., 1::2] = words >> 4
        vals = E2M1[nib]
    vals = vals * np.repeat(np.exp2(scales.astype(np.float64) - 127.0), 8, axis=1)[..., None]
    return vals.transpose(0, 1, 3, 2).reshape(g * 512, n)


def gelu(v):
    return 0.5 * v * (1.0 + np.tanh(np.sqrt(2.0 / np.pi) * (v + 0.044715 * v**3)))


K, K2, H, N, T, S, P, T2 = 1024, 512, 1024, 384, 2048, 1024, 512, 2048

def setup_inputs():
    n = np.random.standard_normal
    s, s2, u = mx_kscale(K)[:, None], mx_kscale(K2)[:, None], mx_kscale(H)[:, None]
    perm = np.random.permutation(T2)
    tab_words, tab_scales = pack_weight(n((K, T)) * s, "e4m3")
    tab2_words, tab2_scales = pack_weight(n((K2, T)) * s2, "e4m3")
    w2_words, w2_scales = pack_weight(0.85 * n((K2, H)) / np.sqrt(K2) / s2 * u.T, "e4m3")
    w4_words, w4_scales = pack_weight(n((H, N)) / np.sqrt(H) / u, "e2m1")
    return {
        "tab_words": tab_words, "tab_scales": tab_scales,
        "tab2_words": tab2_words, "tab2_scales": tab2_scales,
        "offs": striped(np.random.permutation(T)[:S]),
        "offs2": striped(np.random.permutation(T)[:P]),
        "pos1": striped(np.random.permutation(S)[:P]),
        "offs3": striped(perm[:S]),
        "offs4": striped(perm[S:S + P]),
        "w1": (0.85 * n((K, H)) / np.sqrt(K) / s * u.T).astype(np.float32),
        "w2_words": w2_words, "w2_scales": w2_scales,
        "rate": (np.random.uniform(0.3, 0.65, H) / u[:, 0]).astype(np.float32),
        "w3": (n((H, N)) / np.sqrt(H) / u).astype(np.float32),
        "w4_words": w4_words, "w4_scales": w4_scales,
        "b": (0.8 * n(N)).astype(np.float32),
        "wg1": np.exp(0.3 * n((128, S))).astype(np.float32),
        "wg2": np.exp(0.3 * n((128, P))).astype(np.float32),
        "page1": (0.8 * n((N, T2))).astype(np.float32)}

def reference(tab_words, tab_scales, tab2_words, tab2_scales, offs, offs2, pos1, offs3, offs4, w1, w2_words, w2_scales, rate, w3, w4_words, w4_scales, b, wg1, wg2, page1):
    v = unpack_weight(tab_words, tab_scales, "e4m3")[:, unstriped(offs)]
    v2 = unpack_weight(tab2_words, tab2_scales, "e4m3")[:, unstriped(offs2)]
    h1 = mxq(f64(w1), 0, "e4m3").T @ v
    h2 = unpack_weight(w2_words, w2_scales, "e4m3").T @ v2
    z1 = h1 * np.cos(f64(rate)[:, None] * h1)
    z2 = np.maximum(h2, h1[:, unstriped(pos1)])
    y1 = mxq(f64(w3), 0, "e4m3").T @ mxq(z1, 0, "e4m3")
    y2 = (unpack_weight(w4_words, w4_scales, "e2m1").T @ mxq(z2, 0, "e4m3")) + f64(b)[:, None]
    out = f64(page1).copy()
    out[:, unstriped(offs3)] = np.tile(f64(wg1), (N // 128, 1)) * y1
    out[:, unstriped(offs4)] = np.tile(f64(wg2), (N // 128, 1)) * y2
    return out

@@ -1,0 +1,333 @@
+import math
+from contextlib import ExitStack
+
+import concourse.mybir as mybir
+
+K, K2, H, N, T, S, P2, T2 = 1024, 512, 1024, 384, 2048, 1024, 512, 2048
+FLOPS = 2 * (K * H * S + K2 * H * P2 + H * N * S + H * N * P2)
+
+F32 = mybir.dt.float32
+BF16 = mybir.dt.bfloat16
+I32 = mybir.dt.int32
+U32 = mybir.dt.uint32
+U16 = mybir.dt.uint16
+U8 = mybir.dt.uint8
+FP8X4 = mybir.dt.float8_e4m3fn_x4
+FP4X4 = mybir.dt.float4_e2m1fn_x4
+ALU = mybir.AluOpType
+ACT = mybir.ActivationFunctionType
+
+PART = 128
+PACK = 4
+PASS = PART * PACK
+BANK = 512
+QUADS = 4
+LIST_ROWS = 16
+
+
+def tile_list_slotting_effort_scores_kernel(
+    tc, tab_words, tab_scales, tab2_words, tab2_scales, offs, offs2, pos1, offs3, offs4,
+    w1, w2_words, w2_scales, rate, w3, w4_words, w4_scales, b, wg1, wg2, page1, out,
+):
+    nc = tc.nc
+    k_passes = K // PASS
+    r_passes = H // PASS
+    n_tiles = N // PART
+    chunks = S // BANK
+
+    with ExitStack() as ctx:
+        keep = ctx.enter_context(tc.tile_pool(name="keep", bufs=1))
+        raw_pool = ctx.enter_context(tc.tile_pool(name="raw", bufs=3))
+        ring = ctx.enter_context(tc.tile_pool(name="ring", bufs=2))
+        z_pool = ctx.enter_context(tc.tile_pool(name="zq", bufs=4))
+        psum_h1 = ctx.enter_context(tc.psum_pool(name="psum_h1", bufs=3))
+        psum_h2 = ctx.enter_context(tc.psum_pool(name="psum_h2", bufs=2))
+        psum_y = ctx.enter_context(tc.psum_pool(name="psum_y", bufs=3))
+
+        def kept(shape, dtype, name):
+            return keep.tile(shape, dtype, name=name, align_bytes=64)
+
+        def load_list(src, name):
+            tile = kept([PART, src.shape[1]], U16, name)
+            nc.sync.dma_start(tile[:], src)
+            return tile
+
+        def load_words(src, name):
+            tile = kept([PART, src.shape[1]], I32, name)
+            nc.sync.dma_start(out=tile[:], in_=src.rearrange("p t i -> p (t i)").bitcast(I32))
+            return tile
+
+        def load_raw(src, name):
+            tile = raw_pool.tile([PART, PACK, src.shape[1]], F32, name=name, tag="raw", align_bytes=64)
+            nc.sync.dma_start(out=tile[:], in_=src.rearrange("(p j) c -> p j c", j=PACK))
+            return tile
+
+        def quantize(grouped, codes, scales):
+            nc.vector.quantize_mx(
+                out=codes[:].bitcast(FP8X4), scales=scales[:], in_=grouped[:].rearrange("p c j -> p (c j)")
+            )
+
+        tab_sc = kept([PART, T], U8, "tab_sc")
+        tab2_sc = kept([PART, T], U8, "tab2_sc")
+        w2_sc_raw = kept([PART, H], U8, "w2_sc_raw")
+        w4_sc = kept([PART, r_passes, N], U8, "w4_sc")
+        nc.vector.memset(tab_sc[:].bitcast(I32), 0)
+        nc.gpsimd.memset(tab2_sc[:].bitcast(I32), 0)
+        nc.gpsimd.memset(w2_sc_raw[:].bitcast(I32), 0)
+        nc.gpsimd.memset(w4_sc[:].bitcast(I32), 0)
+        one = kept([PART, 1], F32, "one")
+        half_pi = kept([PART, 1], F32, "half_pi")
+        nc.gpsimd.memset(one[:], 1.0)
+        nc.gpsimd.tensor_scalar(half_pi[:], one[:], math.pi / 2, 0.0, ALU.mult, ALU.add)
+
+        w1_raw = {}
+        idx = load_list(offs, "idx")
+        for q in range(QUADS):
+            nc.sync.dma_start(
+                out=tab_sc[32 * q : 32 * q + 4 * k_passes, :].bitcast(I32),
+                in_=tab_scales[:, 4 * q : 4 * q + 4, :].bitcast(I32),
+            )
+        tab_w = [load_words(tab_words[0], "tab_w0")]
+        tab_w.append(load_words(tab_words[1], "tab_w1"))
+        w1_raw[0, 0] = load_raw(w1[0:PASS, 0:PASS], "w1_raw00")
+        w1_raw[1, 0] = load_raw(w1[PASS : 2 * PASS, 0:PASS], "w1_raw10")
+        idx2 = load_list(offs2, "idx2")
+        tab2_w = load_words(tab2_words[0], "tab2_w")
+        p1 = load_list(pos1, "p1")
+        w2_raw = load_words(w2_words[0], "w2_raw")
+
+        for q in range(QUADS):
+            nc.gpsimd.dma_start(
+                out=tab2_sc[32 * q : 32 * q + 4, :].bitcast(I32),
+                in_=tab2_scales[0, 4 * q : 4 * q + 4, :].bitcast(I32),
+            )
+        for q in range(QUADS):
+            nc.gpsimd.dma_start(
+                out=w2_sc_raw[32 * q : 32 * q + 4, :].bitcast(I32),
+                in_=w2_scales[0, 4 * q : 4 * q + 4, :].bitcast(I32),
+            )
+
+        v_w = [kept([PART, S], U32, "v_w%d" % a) for a in range(k_passes)]
+        v_sc = kept([PART, S], U8, "v_sc")
+        nc.vector.tensor_copy(v_sc[:], tab_sc[:].indirect(idx[:]))
+        nc.vector.tensor_copy(v_w[0][:], tab_w[0][:].bitcast(U32).indirect(idx[:]))
+        nc.vector.tensor_copy(v_w[1][:], tab_w[1][:].bitcast(U32).indirect(idx[:]))
+
+        w1_codes = {}
+        w1_sc = {}
+
+        def quantize_w1(a, g):
+            grouped = ring.tile([PART, PASS, PACK], BF16, name="w_grouped", tag="w_grouped", align_bytes=64)
+            eng = "ASGG"[2 * g + a]
+            if eng == "A":
+                nc.scalar.copy(
+                    out=grouped[:].rearrange("p (t m) j -> p m j t", t=PACK),
+                    in_=w1_raw[a, g][:].rearrange("p j (m t) -> p m j t", t=PACK),
+                )
+            elif eng == "V":
+                nc.vector.tensor_copy(
+                    out=grouped[:].rearrange("p (t m) j -> p m j t", t=PACK),
+                    in_=w1_raw[a, g][:].rearrange("p j (m t) -> p m j t", t=PACK),
+                )
+            elif eng == "S":
+                dst = grouped[:].rearrange("p (t m) j -> p m j t", t=PACK)
+                src = w1_raw[a, g][:].rearrange("p j (m t) -> p m j t", t=PACK)
+                nc.scalar.copy(out=dst[:, :48], in_=src[:, :48])
+                nc.vector.tensor_copy(out=dst[:, 48:], in_=src[:, 48:])
+            else:
+                nc.gpsimd.tensor_scalar(
+                    grouped[:].rearrange("p (t m) j -> p t m j", t=PACK),
+                    w1_raw[a, g][:].rearrange("p j (m t) -> p t m j", t=PACK),
+                    1.0, 0.0, ALU.mult, ALU.add,
+                )
+            w1_codes[a, g] = kept([PART, PASS], U32, "w1_codes%d%d" % (a, g))
+            w1_sc[a, g] = kept([PART, PASS], U8, "w1_sc%d%d" % (a, g))
+            quantize(grouped, w1_codes[a, g], w1_sc[a, g])
+
+        for a in range(k_passes):
+            quantize_w1(a, 0)
+
+        v2_w = kept([PART, P2], U32, "v2_w")
+        v2_sc = kept([PART, P2], U8, "v2_sc")
+        nc.vector.tensor_copy(v2_w[:], tab2_w[:].bitcast(U32).indirect(idx2[:]))
+        nc.vector.tensor_copy(v2_sc[:], tab2_sc[:].indirect(idx2[:]))
+
+        w2_codes = kept([PART, H], I32, "w2_codes")
+        w2_sc = kept([PART, H], U8, "w2_sc")
+        nc.gpsimd.tensor_copy(
+            out=w2_sc[:].rearrange("p (g t m) -> p g t m", g=r_passes, t=PACK),
+            in_=w2_sc_raw[:].rearrange("p (g m t) -> p g t m", g=r_passes, t=PACK),
+        )
+        nc.gpsimd.tensor_copy(
+            out=w2_codes[:].rearrange("p (g t m) -> p g t m", g=r_passes, t=PACK),
+            in_=w2_raw[:].rearrange("p (g m t) -> p g t m", g=r_passes, t=PACK),
+        )
+
+        for a in range(k_passes):
+            w1_raw[a, 1] = load_raw(w1[a * PASS : (a + 1) * PASS, PASS : 2 * PASS], "w1_raw%d1" % a)
+        rate_sb = kept([PART, r_passes, PACK], F32, "rate_sb")
+        nc.sync.dma_start(out=rate_sb[:], in_=rate.rearrange("(g p t) -> p g t", p=PART, t=PACK))
+        w3_raw = [load_raw(w3[g * PASS : (g + 1) * PASS, :], "w3_raw%d" % g) for g in range(r_passes)]
+        w4_w = kept([PART, r_passes, 2 * N], U8, "w4_w")
+        nc.sync.dma_start(out=w4_w[:].bitcast(I32), in_=w4_words.rearrange("a p c -> p a c").bitcast(I32))
+        for q in range(QUADS):
+            nc.sync.dma_start(
+                out=w4_sc[32 * q : 32 * q + 4, :, :].bitcast(I32),
+                in_=w4_scales[:, 4 * q : 4 * q + 4, :].rearrange("a r c -> r a c").bitcast(I32),
+            )
+        wg2_sb = kept([PART, P2], F32, "wg2_sb")
+        nc.sync.dma_start(out=wg2_sb[:], in_=wg2)
+        idx4 = load_list(offs4, "idx4")
+        b_sb = kept([PART, n_tiles], F32, "b_sb")
+        with nc.allow_non_contiguous_dma(reason="one bias value a partition"):
+            nc.sync.dma_start(out=b_sb[:], in_=b.rearrange("(i p) -> p i", p=PART))
+        pages = []
+        for i in range(n_tiles):
+            page = kept([PART, T2], F32, "page%d" % i)
+            nc.sync.dma_start(out=page[:], in_=page1[i * PART : (i + 1) * PART, :])
+            pages.append(page)
+        wg1_sb = kept([PART, S], F32, "wg1_sb")
+        nc.sync.dma_start(out=wg1_sb[:], in_=wg1)
+        idx3 = load_list(offs3, "idx3")
+
+        h1 = [kept([PART, PACK, S], F32, "h1_%d" % g) for g in range(r_passes)]
+        z2_codes = []
+        z2_sc = []
+        for g in range(r_passes):
+            if g > 0:
+                for a in range(k_passes):
+                    quantize_w1(a, g)
+            picked = ring.tile([PART, PACK, P2], F32, name="picked", tag="picked", align_bytes=64)
+            for t in range(PACK):
+                cols = slice(t * PART, (t + 1) * PART)
+                for c in range(chunks):
+                    js = slice(c * BANK, (c + 1) * BANK)
+                    acc = psum_h1.tile([PART, BANK], F32, name="acc_h1", tag="acc_h1")
+                    for a in range(k_passes):
+                        nc.tensor.matmul_mx(
+                            out=acc[:],
+                            lhsT=w1_codes[a, g][:, cols].bitcast(FP8X4),
+                            lhsT_scale=w1_sc[a, g][:, cols],
+                            rhs=v_w[a][:, js].bitcast(FP8X4),
+                            rhs_scale=v_sc[4 * a : PART, js],
+                            start=(a == 0),
+                            stop=(a == k_passes - 1),
+                        )
+                    nc.scalar.copy(out=h1[g][:, t, js], in_=acc[:])
+                nc.vector.tensor_copy(picked[:, t, :], h1[g][:, t, :].indirect(p1[:]))
+
+            z2 = ring.tile([PART, P2, PACK], BF16, name="z2", tag="z", align_bytes=64)
+            for jb in range(P2 // PART):
+                js = slice(jb * PART, (jb + 1) * PART)
+                acc2 = psum_h2.tile([PART, PACK, PART], F32, name="acc_h2", tag="acc_h2")
+                for t in range(PACK):
+                    cols = slice(g * PASS + t * PART, g * PASS + (t + 1) * PART)
+                    nc.tensor.matmul_mx(
+                        out=acc2[:, t, :],
+                        lhsT=w2_codes[:, cols].bitcast(FP8X4),
+                        lhsT_scale=w2_sc[:, cols],
+                        rhs=v2_w[:, js].bitcast(FP8X4),
+                        rhs_scale=v2_sc[:, js],
+                        start=True,
+                        stop=True,
+                    )
+                nc.vector.tensor_tensor(
+                    out=z2[:, js, :].rearrange("p (c i) t -> p c t i", i=PACK),
+                    in0=picked[:, :, js].rearrange("p t (c i) -> p c t i", i=PACK),
+                    in1=acc2[:].rearrange("p t (c i) -> p c t i", i=PACK),
+                    op=ALU.max,
+                )
+            codes = z_pool.tile([PART, P2], U32, name="z2_codes", tag="z_codes", align_bytes=64)
+            scales = z_pool.tile([PART, P2], U8, name="z2_sc", tag="z_sc", align_bytes=64)
+            quantize(z2, codes, scales)
+            z2_codes.append(codes)
+            z2_sc.append(scales)
+
+        y2_acc = []
+        for i in range(n_tiles):
+            acc = psum_y.tile([PART, BANK], F32, name="acc_y2", tag="acc_y")
+            for g in range(r_passes):
+                nc.tensor.matmul_mx(
+                    out=acc[:],
+                    lhsT=w4_w[:, g, 2 * i * PART : 2 * (i + 1) * PART].bitcast(FP4X4),
+                    lhsT_scale=w4_sc[:, g, i * PART : (i + 1) * PART],
+                    rhs=z2_codes[g][:].bitcast(FP8X4),
+                    rhs_scale=z2_sc[g][:],
+                    start=(g == 0),
+                    stop=(g == r_passes - 1),
+                )
+            y2_acc.append(acc)
+
+        cosines = {}
+        z1_codes = {}
+        z1_sc = {}
+
+        def make_z1(c):
+            js = slice(c * BANK, (c + 1) * BANK)
+            for g in range(r_passes):
+                cos = kept([PART, PACK, BANK], F32, "cos%d%d" % (c, g))
+                cosines[c, g] = cos
+                for t in range(PACK):
+                    nc.scalar.activation(
+                        out=cos[:, t, :], in_=h1[g][:, t, js], func=ACT.Abs, scale=rate_sb[:, g, t : t + 1]
+                    )
+                flat = cos[:].rearrange("p t j -> p (t j)")
+                nc.scalar.activation(out=flat, in_=flat, func=ACT.Sin, scale=-1.0, bias=half_pi[:])
+                z1 = ring.tile([PART, BANK, PACK], BF16, name="z1", tag="z", align_bytes=64)
+                nc.vector.tensor_tensor(
+                    out=z1[:].rearrange("p (c i) t -> p c t i", i=PACK),
+                    in0=cos[:].rearrange("p t (c i) -> p c t i", i=PACK),
+                    in1=h1[g][:, :, js].rearrange("p t (c i) -> p c t i", i=PACK),
+                    op=ALU.mult,
+                )
+                z1_codes[c, g] = z_pool.tile([PART, BANK], U32, name="z1_codes", tag="z_codes", align_bytes=64)
+                z1_sc[c, g] = z_pool.tile([PART, BANK], U8, name="z1_sc", tag="z_sc", align_bytes=64)
+                quantize(z1, z1_codes[c, g], z1_sc[c, g])
+
+        make_z1(0)
+
+        w3_codes = []
+        w3_sc = []
+        for g in range(r_passes):
+            grouped = ring.tile([PART, N, PACK], BF16, name="w3_grouped", tag="w_grouped", align_bytes=64)
+            nc.gpsimd.tensor_scalar(
+                grouped[:], w3_raw[g][:].rearrange("p j c -> p c j"), 1.0, 0.0, ALU.mult, ALU.add
+            )
+            w3_codes.append(kept([PART, N], U32, "w3_codes%d" % g))
+            w3_sc.append(kept([PART, N], U8, "w3_sc%d" % g))
+            quantize(grouped, w3_codes[g], w3_sc[g])
+
+        staged = cosines[0, 1]
+        for i in range(n_tiles):
+            nc.scalar.activation(
+                out=staged[:, i, :], in_=y2_acc[i][:], func=ACT.Identity, bias=b_sb[:, i : i + 1]
+            )
+            nc.vector.tensor_tensor(
+                out=pages[i][:].indirect(idx4[:]), in0=staged[:, i, :], in1=wg2_sb[:], op=ALU.mult
+            )
+
+        make_z1(1)
+
+        for c in range(chunks):
+            js = slice(c * BANK, (c + 1) * BANK)
+            entries = idx3[:, c * BANK // LIST_ROWS : (c + 1) * BANK // LIST_ROWS]
+            staged = cosines[1, 1 - c]
+            for i in range(n_tiles):
+                cols = slice(i * PART, (i + 1) * PART)
+                acc = psum_y.tile([PART, BANK], F32, name="acc_y1", tag="acc_y")
+                for g in range(r_passes):
+                    nc.tensor.matmul_mx(
+                        out=acc[:],
+                        lhsT=w3_codes[g][:, cols].bitcast(FP8X4),
+                        lhsT_scale=w3_sc[g][:, cols],
+                        rhs=z1_codes[c, g][:].bitcast(FP8X4),
+                        rhs_scale=z1_sc[c, g][:],
+                        start=(g == 0),
+                        stop=(g == r_passes - 1),
+                    )
+                nc.scalar.copy(out=staged[:, i, :], in_=acc[:])
+                nc.vector.tensor_tensor(
+                    out=pages[i][:].indirect(entries), in0=staged[:, i, :], in1=wg1_sb[:, js], op=ALU.mult
+                )
+                if c == chunks - 1:
+                    nc.sync.dma_start(out=out[i * PART : (i + 1) * PART, :], in_=pages[i][:])

@@ -40,9 +40,8 @@ def tile_list_slotting_effort_scores_kernel(
         raw_pool = ctx.enter_context(tc.tile_pool(name="raw", bufs=3))
         ring = ctx.enter_context(tc.tile_pool(name="ring", bufs=2))
         z_pool = ctx.enter_context(tc.tile_pool(name="zq", bufs=4))
-        psum_h1 = ctx.enter_context(tc.psum_pool(name="psum_h1", bufs=3))
-        psum_h2 = ctx.enter_context(tc.psum_pool(name="psum_h2", bufs=2))
-        psum_y = ctx.enter_context(tc.psum_pool(name="psum_y", bufs=3))
+        psum_h1 = ctx.enter_context(tc.psum_pool(name="psum_h1", bufs=4))
+        psum_y = ctx.enter_context(tc.psum_pool(name="psum_y", bufs=4))
 
         def kept(shape, dtype, name):
             return keep.tile(shape, dtype, name=name, align_bytes=64)
@@ -82,35 +81,35 @@ def tile_list_slotting_effort_scores_kernel(
 
         w1_raw = {}
         idx = load_list(offs, "idx")
+        tab_w = [load_words(tab_words[0], "tab_w0")]
         for q in range(QUADS):
             nc.sync.dma_start(
                 out=tab_sc[32 * q : 32 * q + 4 * k_passes, :].bitcast(I32),
                 in_=tab_scales[:, 4 * q : 4 * q + 4, :].bitcast(I32),
             )
-        tab_w = [load_words(tab_words[0], "tab_w0")]
         tab_w.append(load_words(tab_words[1], "tab_w1"))
         w1_raw[0, 0] = load_raw(w1[0:PASS, 0:PASS], "w1_raw00")
         w1_raw[1, 0] = load_raw(w1[PASS : 2 * PASS, 0:PASS], "w1_raw10")
+        for q in range(QUADS):
+            nc.sync.dma_start(
+                out=tab2_sc[32 * q : 32 * q + 4, :].bitcast(I32),
+                in_=tab2_scales[0, 4 * q : 4 * q + 4, :].bitcast(I32),
+            )
         idx2 = load_list(offs2, "idx2")
         tab2_w = load_words(tab2_words[0], "tab2_w")
         p1 = load_list(pos1, "p1")
         w2_raw = load_words(w2_words[0], "w2_raw")
 
         for q in range(QUADS):
-            nc.gpsimd.dma_start(
-                out=tab2_sc[32 * q : 32 * q + 4, :].bitcast(I32),
-                in_=tab2_scales[0, 4 * q : 4 * q + 4, :].bitcast(I32),
-            )
-        for q in range(QUADS):
-            nc.gpsimd.dma_start(
+            nc.sync.dma_start(
                 out=w2_sc_raw[32 * q : 32 * q + 4, :].bitcast(I32),
                 in_=w2_scales[0, 4 * q : 4 * q + 4, :].bitcast(I32),
             )
 
         v_w = [kept([PART, S], U32, "v_w%d" % a) for a in range(k_passes)]
         v_sc = kept([PART, S], U8, "v_sc")
-        nc.vector.tensor_copy(v_sc[:], tab_sc[:].indirect(idx[:]))
         nc.vector.tensor_copy(v_w[0][:], tab_w[0][:].bitcast(U32).indirect(idx[:]))
+        nc.vector.tensor_copy(v_sc[:], tab_sc[:].indirect(idx[:]))
         nc.vector.tensor_copy(v_w[1][:], tab_w[1][:].bitcast(U32).indirect(idx[:]))
 
         w1_codes = {}
@@ -118,7 +117,7 @@ def tile_list_slotting_effort_scores_kernel(
 
         def quantize_w1(a, g):
             grouped = ring.tile([PART, PASS, PACK], BF16, name="w_grouped", tag="w_grouped", align_bytes=64)
-            eng = "ASGG"[2 * g + a]
+            eng = "ASAV"[2 * g + a]
             if eng == "A":
                 nc.scalar.copy(
                     out=grouped[:].rearrange("p (t m) j -> p m j t", t=PACK),
@@ -219,7 +218,7 @@ def tile_list_slotting_effort_scores_kernel(
             z2 = ring.tile([PART, P2, PACK], BF16, name="z2", tag="z", align_bytes=64)
             for jb in range(P2 // PART):
                 js = slice(jb * PART, (jb + 1) * PART)
-                acc2 = psum_h2.tile([PART, PACK, PART], F32, name="acc_h2", tag="acc_h2")
+                acc2 = psum_y.tile([PART, PACK, PART], F32, name="acc_h2", tag="acc_y")
                 for t in range(PACK):
                     cols = slice(g * PASS + t * PART, g * PASS + (t + 1) * PART)
                     nc.tensor.matmul_mx(
@@ -271,8 +270,10 @@ def tile_list_slotting_effort_scores_kernel(
                     nc.scalar.activation(
                         out=cos[:, t, :], in_=h1[g][:, t, js], func=ACT.Abs, scale=rate_sb[:, g, t : t + 1]
                     )
-                flat = cos[:].rearrange("p t j -> p (t j)")
-                nc.scalar.activation(out=flat, in_=flat, func=ACT.Sin, scale=-1.0, bias=half_pi[:])
+                for t in range(PACK):
+                    nc.scalar.activation(
+                        out=cos[:, t, :], in_=cos[:, t, :], func=ACT.Sin, scale=-1.0, bias=half_pi[:]
+                    )
                 z1 = ring.tile([PART, BANK, PACK], BF16, name="z1", tag="z", align_bytes=64)
                 nc.vector.tensor_tensor(
                     out=z1[:].rearrange("p (c i) t -> p c t i", i=PACK),
@@ -290,8 +291,9 @@ def tile_list_slotting_effort_scores_kernel(
         w3_sc = []
         for g in range(r_passes):
             grouped = ring.tile([PART, N, PACK], BF16, name="w3_grouped", tag="w_grouped", align_bytes=64)
-            nc.gpsimd.tensor_scalar(
-                grouped[:], w3_raw[g][:].rearrange("p j c -> p c j"), 1.0, 0.0, ALU.mult, ALU.add
+            nc.scalar.copy(
+                out=grouped[:].rearrange("p (c i) j -> p c j i", i=PACK),
+                in_=w3_raw[g][:].rearrange("p j (c i) -> p c j i", i=PACK),
             )
             w3_codes.append(kept([PART, N], U32, "w3_codes%d" % g))
             w3_sc.append(kept([PART, N], U8, "w3_sc%d" % g))
@@ -311,7 +313,6 @@ def tile_list_slotting_effort_scores_kernel(
         for c in range(chunks):
             js = slice(c * BANK, (c + 1) * BANK)
             entries = idx3[:, c * BANK // LIST_ROWS : (c + 1) * BANK // LIST_ROWS]
-            staged = cosines[1, 1 - c]
             for i in range(n_tiles):
                 cols = slice(i * PART, (i + 1) * PART)
                 acc = psum_y.tile([PART, BANK], F32, name="acc_y1", tag="acc_y")
@@ -325,6 +326,7 @@ def tile_list_slotting_effort_scores_kernel(
                         start=(g == 0),
                         stop=(g == r_passes - 1),
                     )
+                staged = cosines[1, 1 if i == n_tiles - 1 else 0] if c == 0 else cosines[0, 0]
                 nc.scalar.copy(out=staged[:, i, :], in_=acc[:])
                 nc.vector.tensor_tensor(
                     out=pages[i][:].indirect(entries), in0=staged[:, i, :], in1=wg1_sb[:, js], op=ALU.mult

@@ -3,8 +3,8 @@ from contextlib import ExitStack
 
 import concourse.mybir as mybir
 
-K, K2, H, N, T, S, P2, T2 = 1024, 512, 1024, 384, 2048, 1024, 512, 2048
-FLOPS = 2 * (K * H * S + K2 * H * P2 + H * N * S + H * N * P2)
+K, K2, H, N, T, S, S2, T2 = 1024, 512, 1024, 384, 2048, 1024, 512, 2048
+FLOPS = 2 * (K * H * S + K2 * H * S2 + H * N * S + H * N * S2)
 
 F32 = mybir.dt.float32
 BF16 = mybir.dt.bfloat16
@@ -22,7 +22,11 @@ PACK = 4
 PASS = PART * PACK
 BANK = 512
 QUADS = 4
+QUAD = PART // QUADS
+SCALE_ROWS = 4
 LIST_ROWS = 16
+LINE = 4
+SCALAR_SHARE = 48
 
 
 def tile_list_slotting_effort_scores_kernel(
@@ -31,7 +35,7 @@ def tile_list_slotting_effort_scores_kernel(
 ):
     nc = tc.nc
     k_passes = K // PASS
-    r_passes = H // PASS
+    groups = H // PASS
     n_tiles = N // PART
     chunks = S // BANK
 
@@ -39,9 +43,9 @@ def tile_list_slotting_effort_scores_kernel(
         keep = ctx.enter_context(tc.tile_pool(name="keep", bufs=1))
         raw_pool = ctx.enter_context(tc.tile_pool(name="raw", bufs=3))
         ring = ctx.enter_context(tc.tile_pool(name="ring", bufs=2))
-        z_pool = ctx.enter_context(tc.tile_pool(name="zq", bufs=4))
+        z_pool = ctx.enter_context(tc.tile_pool(name="zq", bufs=2 * groups))
         psum_h1 = ctx.enter_context(tc.psum_pool(name="psum_h1", bufs=4))
-        psum_y = ctx.enter_context(tc.psum_pool(name="psum_y", bufs=4))
+        psum_rest = ctx.enter_context(tc.psum_pool(name="psum_rest", bufs=4))
 
         def kept(shape, dtype, name):
             return keep.tile(shape, dtype, name=name, align_bytes=64)
@@ -56,6 +60,14 @@ def tile_list_slotting_effort_scores_kernel(
             nc.sync.dma_start(out=tile[:], in_=src.rearrange("p t i -> p (t i)").bitcast(I32))
             return tile
 
+        def load_scale_rows(tile, src):
+            rows = SCALE_ROWS * src.shape[0]
+            for quad in range(QUADS):
+                nc.sync.dma_start(
+                    out=tile[QUAD * quad : QUAD * quad + rows, :].bitcast(I32),
+                    in_=src[:, SCALE_ROWS * quad : SCALE_ROWS * (quad + 1), :].bitcast(I32),
+                )
+
         def load_raw(src, name):
             tile = raw_pool.tile([PART, PACK, src.shape[1]], F32, name=name, tag="raw", align_bytes=64)
             nc.sync.dma_start(out=tile[:], in_=src.rearrange("(p j) c -> p j c", j=PACK))
@@ -66,10 +78,16 @@ def tile_list_slotting_effort_scores_kernel(
                 out=codes[:].bitcast(FP8X4), scales=scales[:], in_=grouped[:].rearrange("p c j -> p (c j)")
             )
 
+        def by_lines(planes):
+            return planes.rearrange("p t (c i) -> p c t i", i=LINE)
+
+        def by_lines_interleaved(grouped):
+            return grouped.rearrange("p (c i) t -> p c t i", i=LINE)
+
         tab_sc = kept([PART, T], U8, "tab_sc")
         tab2_sc = kept([PART, T], U8, "tab2_sc")
         w2_sc_raw = kept([PART, H], U8, "w2_sc_raw")
-        w4_sc = kept([PART, r_passes, N], U8, "w4_sc")
+        w4_sc = kept([PART, groups, N], U8, "w4_sc")
         nc.vector.memset(tab_sc[:].bitcast(I32), 0)
         nc.gpsimd.memset(tab2_sc[:].bitcast(I32), 0)
         nc.gpsimd.memset(w2_sc_raw[:].bitcast(I32), 0)
@@ -82,29 +100,16 @@ def tile_list_slotting_effort_scores_kernel(
         w1_raw = {}
         idx = load_list(offs, "idx")
         tab_w = [load_words(tab_words[0], "tab_w0")]
-        for q in range(QUADS):
-            nc.sync.dma_start(
-                out=tab_sc[32 * q : 32 * q + 4 * k_passes, :].bitcast(I32),
-                in_=tab_scales[:, 4 * q : 4 * q + 4, :].bitcast(I32),
-            )
+        load_scale_rows(tab_sc, tab_scales)
         tab_w.append(load_words(tab_words[1], "tab_w1"))
-        w1_raw[0, 0] = load_raw(w1[0:PASS, 0:PASS], "w1_raw00")
-        w1_raw[1, 0] = load_raw(w1[PASS : 2 * PASS, 0:PASS], "w1_raw10")
-        for q in range(QUADS):
-            nc.sync.dma_start(
-                out=tab2_sc[32 * q : 32 * q + 4, :].bitcast(I32),
-                in_=tab2_scales[0, 4 * q : 4 * q + 4, :].bitcast(I32),
-            )
+        for a in range(k_passes):
+            w1_raw[a, 0] = load_raw(w1[a * PASS : (a + 1) * PASS, 0:PASS], "w1_raw%d0" % a)
+        load_scale_rows(tab2_sc, tab2_scales)
         idx2 = load_list(offs2, "idx2")
+        w2_raw = load_words(w2_words[0], "w2_raw")
         tab2_w = load_words(tab2_words[0], "tab2_w")
         p1 = load_list(pos1, "p1")
-        w2_raw = load_words(w2_words[0], "w2_raw")
-
-        for q in range(QUADS):
-            nc.sync.dma_start(
-                out=w2_sc_raw[32 * q : 32 * q + 4, :].bitcast(I32),
-                in_=w2_scales[0, 4 * q : 4 * q + 4, :].bitcast(I32),
-            )
+        load_scale_rows(w2_sc_raw, w2_scales)
 
         v_w = [kept([PART, S], U32, "v_w%d" % a) for a in range(k_passes)]
         v_sc = kept([PART, S], U8, "v_sc")
@@ -114,31 +119,18 @@ def tile_list_slotting_effort_scores_kernel(
 
         w1_codes = {}
         w1_sc = {}
+        w1_grouped = {}
 
         def quantize_w1(a, g):
             grouped = ring.tile([PART, PASS, PACK], BF16, name="w_grouped", tag="w_grouped", align_bytes=64)
-            eng = "ASAV"[2 * g + a]
-            if eng == "A":
-                nc.scalar.copy(
-                    out=grouped[:].rearrange("p (t m) j -> p m j t", t=PACK),
-                    in_=w1_raw[a, g][:].rearrange("p j (m t) -> p m j t", t=PACK),
-                )
-            elif eng == "V":
-                nc.vector.tensor_copy(
-                    out=grouped[:].rearrange("p (t m) j -> p m j t", t=PACK),
-                    in_=w1_raw[a, g][:].rearrange("p j (m t) -> p m j t", t=PACK),
-                )
-            elif eng == "S":
-                dst = grouped[:].rearrange("p (t m) j -> p m j t", t=PACK)
-                src = w1_raw[a, g][:].rearrange("p j (m t) -> p m j t", t=PACK)
-                nc.scalar.copy(out=dst[:, :48], in_=src[:, :48])
-                nc.vector.tensor_copy(out=dst[:, 48:], in_=src[:, 48:])
+            dst = grouped[:].rearrange("p (t m) j -> p m j t", t=PACK)
+            src = w1_raw[a, g][:].rearrange("p j (m t) -> p m j t", t=PACK)
+            if a < k_passes - 1:
+                nc.scalar.copy(out=dst, in_=src)
             else:
-                nc.gpsimd.tensor_scalar(
-                    grouped[:].rearrange("p (t m) j -> p t m j", t=PACK),
-                    w1_raw[a, g][:].rearrange("p j (m t) -> p t m j", t=PACK),
-                    1.0, 0.0, ALU.mult, ALU.add,
-                )
+                nc.scalar.copy(out=dst[:, :SCALAR_SHARE], in_=src[:, :SCALAR_SHARE])
+                nc.vector.tensor_copy(out=dst[:, SCALAR_SHARE:], in_=src[:, SCALAR_SHARE:])
+            w1_grouped[a, g] = grouped
             w1_codes[a, g] = kept([PART, PASS], U32, "w1_codes%d%d" % (a, g))
             w1_sc[a, g] = kept([PART, PASS], U8, "w1_sc%d%d" % (a, g))
             quantize(grouped, w1_codes[a, g], w1_sc[a, g])
@@ -146,35 +138,36 @@ def tile_list_slotting_effort_scores_kernel(
         for a in range(k_passes):
             quantize_w1(a, 0)
 
-        v2_w = kept([PART, P2], U32, "v2_w")
-        v2_sc = kept([PART, P2], U8, "v2_sc")
+        v2_w = kept([PART, S2], U32, "v2_w")
+        v2_sc = kept([PART, S2], U8, "v2_sc")
         nc.vector.tensor_copy(v2_w[:], tab2_w[:].bitcast(U32).indirect(idx2[:]))
         nc.vector.tensor_copy(v2_sc[:], tab2_sc[:].indirect(idx2[:]))
 
-        w2_codes = kept([PART, H], I32, "w2_codes")
+        w2_codes = kept([PART, H], U32, "w2_codes")
         w2_sc = kept([PART, H], U8, "w2_sc")
-        nc.gpsimd.tensor_copy(
-            out=w2_sc[:].rearrange("p (g t m) -> p g t m", g=r_passes, t=PACK),
-            in_=w2_sc_raw[:].rearrange("p (g m t) -> p g t m", g=r_passes, t=PACK),
+        nc.vector.tensor_copy(
+            out=w2_sc[:].rearrange("p (g t m) -> p g m t", g=groups, t=PACK),
+            in_=w2_sc_raw[:].rearrange("p (g m t) -> p g m t", g=groups, t=PACK),
         )
-        nc.gpsimd.tensor_copy(
-            out=w2_codes[:].rearrange("p (g t m) -> p g t m", g=r_passes, t=PACK),
-            in_=w2_raw[:].rearrange("p (g m t) -> p g t m", g=r_passes, t=PACK),
+        nc.scalar.copy(
+            out=w2_codes[:].rearrange("p (g t m) -> p g m t", g=groups, t=PACK),
+            in_=w2_raw[:].bitcast(U32).rearrange("p (g m t) -> p g m t", g=groups, t=PACK),
         )
 
         for a in range(k_passes):
             w1_raw[a, 1] = load_raw(w1[a * PASS : (a + 1) * PASS, PASS : 2 * PASS], "w1_raw%d1" % a)
-        rate_sb = kept([PART, r_passes, PACK], F32, "rate_sb")
+        rate_sb = kept([PART, groups, PACK], F32, "rate_sb")
         nc.sync.dma_start(out=rate_sb[:], in_=rate.rearrange("(g p t) -> p g t", p=PART, t=PACK))
-        w3_raw = [load_raw(w3[g * PASS : (g + 1) * PASS, :], "w3_raw%d" % g) for g in range(r_passes)]
-        w4_w = kept([PART, r_passes, 2 * N], U8, "w4_w")
+        w3_raw = [load_raw(w3[g * PASS : (g + 1) * PASS, :], "w3_raw%d" % g) for g in range(groups)]
+        w4_w = kept([PART, groups, 2 * N], U8, "w4_w")
         nc.sync.dma_start(out=w4_w[:].bitcast(I32), in_=w4_words.rearrange("a p c -> p a c").bitcast(I32))
-        for q in range(QUADS):
+        for quad in range(QUADS):
+            rows = w4_scales[:, SCALE_ROWS * quad : SCALE_ROWS * (quad + 1), :]
             nc.sync.dma_start(
-                out=w4_sc[32 * q : 32 * q + 4, :, :].bitcast(I32),
-                in_=w4_scales[:, 4 * q : 4 * q + 4, :].rearrange("a r c -> r a c").bitcast(I32),
+                out=w4_sc[QUAD * quad : QUAD * quad + SCALE_ROWS, :, :].bitcast(I32),
+                in_=rows.rearrange("a r c -> r a c").bitcast(I32),
             )
-        wg2_sb = kept([PART, P2], F32, "wg2_sb")
+        wg2_sb = kept([PART, S2], F32, "wg2_sb")
         nc.sync.dma_start(out=wg2_sb[:], in_=wg2)
         idx4 = load_list(offs4, "idx4")
         b_sb = kept([PART, n_tiles], F32, "b_sb")
@@ -189,63 +182,65 @@ def tile_list_slotting_effort_scores_kernel(
         nc.sync.dma_start(out=wg1_sb[:], in_=wg1)
         idx3 = load_list(offs3, "idx3")
 
-        h1 = [kept([PART, PACK, S], F32, "h1_%d" % g) for g in range(r_passes)]
+        h1 = [kept([PART, PACK, S], F32, "h1_%d" % g) for g in range(groups)]
         z2_codes = []
         z2_sc = []
-        for g in range(r_passes):
-            if g > 0:
-                for a in range(k_passes):
-                    quantize_w1(a, g)
-            picked = ring.tile([PART, PACK, P2], F32, name="picked", tag="picked", align_bytes=64)
+        for g in range(groups):
+            picked = ring.tile([PART, PACK, S2], F32, name="picked", tag="picked", align_bytes=64)
             for t in range(PACK):
-                cols = slice(t * PART, (t + 1) * PART)
+                places = slice(t * PART, (t + 1) * PART)
                 for c in range(chunks):
                     js = slice(c * BANK, (c + 1) * BANK)
                     acc = psum_h1.tile([PART, BANK], F32, name="acc_h1", tag="acc_h1")
                     for a in range(k_passes):
                         nc.tensor.matmul_mx(
                             out=acc[:],
-                            lhsT=w1_codes[a, g][:, cols].bitcast(FP8X4),
-                            lhsT_scale=w1_sc[a, g][:, cols],
+                            lhsT=w1_codes[a, g][:, places].bitcast(FP8X4),
+                            lhsT_scale=w1_sc[a, g][:, places],
                             rhs=v_w[a][:, js].bitcast(FP8X4),
-                            rhs_scale=v_sc[4 * a : PART, js],
+                            rhs_scale=v_sc[SCALE_ROWS * a : PART, js],
                             start=(a == 0),
                             stop=(a == k_passes - 1),
                         )
                     nc.scalar.copy(out=h1[g][:, t, js], in_=acc[:])
                 nc.vector.tensor_copy(picked[:, t, :], h1[g][:, t, :].indirect(p1[:]))
 
-            z2 = ring.tile([PART, P2, PACK], BF16, name="z2", tag="z", align_bytes=64)
-            for jb in range(P2 // PART):
-                js = slice(jb * PART, (jb + 1) * PART)
-                acc2 = psum_y.tile([PART, PACK, PART], F32, name="acc_h2", tag="acc_y")
+            if g + 1 < groups:
+                for a in range(k_passes):
+                    quantize_w1(a, g + 1)
+                z2 = w1_grouped[0, g + 1]
+            else:
+                z2 = ring.tile([PART, S2, PACK], BF16, name="z2", tag="z", align_bytes=64)
+            for j0 in range(0, S2, PART):
+                js = slice(j0, j0 + PART)
+                acc = psum_rest.tile([PART, PACK, PART], F32, name="acc_h2", tag="acc")
                 for t in range(PACK):
-                    cols = slice(g * PASS + t * PART, g * PASS + (t + 1) * PART)
+                    places = slice(g * PASS + t * PART, g * PASS + (t + 1) * PART)
                     nc.tensor.matmul_mx(
-                        out=acc2[:, t, :],
-                        lhsT=w2_codes[:, cols].bitcast(FP8X4),
-                        lhsT_scale=w2_sc[:, cols],
+                        out=acc[:, t, :],
+                        lhsT=w2_codes[:, places].bitcast(FP8X4),
+                        lhsT_scale=w2_sc[:, places],
                         rhs=v2_w[:, js].bitcast(FP8X4),
                         rhs_scale=v2_sc[:, js],
                         start=True,
                         stop=True,
                     )
                 nc.vector.tensor_tensor(
-                    out=z2[:, js, :].rearrange("p (c i) t -> p c t i", i=PACK),
-                    in0=picked[:, :, js].rearrange("p t (c i) -> p c t i", i=PACK),
-                    in1=acc2[:].rearrange("p t (c i) -> p c t i", i=PACK),
+                    out=by_lines_interleaved(z2[:, js, :]),
+                    in0=by_lines(picked[:, :, js]),
+                    in1=by_lines(acc[:]),
                     op=ALU.max,
                 )
-            codes = z_pool.tile([PART, P2], U32, name="z2_codes", tag="z_codes", align_bytes=64)
-            scales = z_pool.tile([PART, P2], U8, name="z2_sc", tag="z_sc", align_bytes=64)
+            codes = z_pool.tile([PART, S2], U32, name="z2_codes", tag="z_codes", align_bytes=64)
+            scales = z_pool.tile([PART, S2], U8, name="z2_sc", tag="z_sc", align_bytes=64)
             quantize(z2, codes, scales)
             z2_codes.append(codes)
             z2_sc.append(scales)
 
         y2_acc = []
         for i in range(n_tiles):
-            acc = psum_y.tile([PART, BANK], F32, name="acc_y2", tag="acc_y")
-            for g in range(r_passes):
+            acc = psum_rest.tile([PART, BANK], F32, name="acc_y2", tag="acc")
+            for g in range(groups):
                 nc.tensor.matmul_mx(
                     out=acc[:],
                     lhsT=w4_w[:, g, 2 * i * PART : 2 * (i + 1) * PART].bitcast(FP4X4),
@@ -253,7 +248,7 @@ def tile_list_slotting_effort_scores_kernel(
                     rhs=z2_codes[g][:].bitcast(FP8X4),
                     rhs_scale=z2_sc[g][:],
                     start=(g == 0),
-                    stop=(g == r_passes - 1),
+                    stop=(g == groups - 1),
                 )
             y2_acc.append(acc)
 
@@ -263,7 +258,7 @@ def tile_list_slotting_effort_scores_kernel(
 
         def make_z1(c):
             js = slice(c * BANK, (c + 1) * BANK)
-            for g in range(r_passes):
+            for g in range(groups):
                 cos = kept([PART, PACK, BANK], F32, "cos%d%d" % (c, g))
                 cosines[c, g] = cos
                 for t in range(PACK):
@@ -276,9 +271,9 @@ def tile_list_slotting_effort_scores_kernel(
                     )
                 z1 = ring.tile([PART, BANK, PACK], BF16, name="z1", tag="z", align_bytes=64)
                 nc.vector.tensor_tensor(
-                    out=z1[:].rearrange("p (c i) t -> p c t i", i=PACK),
-                    in0=cos[:].rearrange("p t (c i) -> p c t i", i=PACK),
-                    in1=h1[g][:, :, js].rearrange("p t (c i) -> p c t i", i=PACK),
+                    out=by_lines_interleaved(z1[:]),
+                    in0=by_lines(cos[:]),
+                    in1=by_lines(h1[g][:, :, js]),
                     op=ALU.mult,
                 )
                 z1_codes[c, g] = z_pool.tile([PART, BANK], U32, name="z1_codes", tag="z_codes", align_bytes=64)
@@ -289,17 +284,14 @@ def tile_list_slotting_effort_scores_kernel(
 
         w3_codes = []
         w3_sc = []
-        for g in range(r_passes):
+        for g in range(groups):
             grouped = ring.tile([PART, N, PACK], BF16, name="w3_grouped", tag="w_grouped", align_bytes=64)
-            nc.scalar.copy(
-                out=grouped[:].rearrange("p (c i) j -> p c j i", i=PACK),
-                in_=w3_raw[g][:].rearrange("p j (c i) -> p c j i", i=PACK),
-            )
+            nc.scalar.copy(out=by_lines_interleaved(grouped[:]), in_=by_lines(w3_raw[g][:]))
             w3_codes.append(kept([PART, N], U32, "w3_codes%d" % g))
             w3_sc.append(kept([PART, N], U8, "w3_sc%d" % g))
             quantize(grouped, w3_codes[g], w3_sc[g])
 
-        staged = cosines[0, 1]
+        staged = cosines[0, groups - 1]
         for i in range(n_tiles):
             nc.scalar.activation(
                 out=staged[:, i, :], in_=y2_acc[i][:], func=ACT.Identity, bias=b_sb[:, i : i + 1]
@@ -310,26 +302,27 @@ def tile_list_slotting_effort_scores_kernel(
 
         make_z1(1)
 
+        staging = [[cosines[1, 0]] * (n_tiles - 1) + [cosines[1, groups - 1]], [cosines[0, 0]] * n_tiles]
         for c in range(chunks):
             js = slice(c * BANK, (c + 1) * BANK)
             entries = idx3[:, c * BANK // LIST_ROWS : (c + 1) * BANK // LIST_ROWS]
             for i in range(n_tiles):
-                cols = slice(i * PART, (i + 1) * PART)
-                acc = psum_y.tile([PART, BANK], F32, name="acc_y1", tag="acc_y")
-                for g in range(r_passes):
+                ns = slice(i * PART, (i + 1) * PART)
+                acc = psum_rest.tile([PART, BANK], F32, name="acc_y1", tag="acc")
+                for g in range(groups):
                     nc.tensor.matmul_mx(
                         out=acc[:],
-                        lhsT=w3_codes[g][:, cols].bitcast(FP8X4),
-                        lhsT_scale=w3_sc[g][:, cols],
+                        lhsT=w3_codes[g][:, ns].bitcast(FP8X4),
+                        lhsT_scale=w3_sc[g][:, ns],
                         rhs=z1_codes[c, g][:].bitcast(FP8X4),
                         rhs_scale=z1_sc[c, g][:],
                         start=(g == 0),
-                        stop=(g == r_passes - 1),
+                        stop=(g == groups - 1),
                     )
-                staged = cosines[1, 1 if i == n_tiles - 1 else 0] if c == 0 else cosines[0, 0]
+                staged = staging[c][i]
                 nc.scalar.copy(out=staged[:, i, :], in_=acc[:])
                 nc.vector.tensor_tensor(
                     out=pages[i][:].indirect(entries), in0=staged[:, i, :], in1=wg1_sb[:, js], op=ALU.mult
                 )
                 if c == chunks - 1:
-                    nc.sync.dma_start(out=out[i * PART : (i + 1) * PART, :], in_=pages[i][:])
+                    nc.sync.dma_start(out=out[ns, :], in_=pages[i][:])

@@ -96,6 +96,8 @@ def tile_list_slotting_effort_scores_kernel(
         half_pi = kept([PART, 1], F32, "half_pi")
         nc.gpsimd.memset(one[:], 1.0)
         nc.gpsimd.tensor_scalar(half_pi[:], one[:], math.pi / 2, 0.0, ALU.mult, ALU.add)
+        warm = kept([PART, 1], F32, "warm")
+        nc.scalar.activation(out=warm[:], in_=one[:], func=ACT.Sin)
 
         w1_raw = {}
         idx = load_list(offs, "idx")

import math
from contextlib import ExitStack

import concourse.mybir as mybir

K, K2, H, N, T, S, S2, T2 = 1024, 512, 1024, 384, 2048, 1024, 512, 2048
FLOPS = 2 * (K * H * S + K2 * H * S2 + H * N * S + H * N * S2)

F32 = mybir.dt.float32
BF16 = mybir.dt.bfloat16
I32 = mybir.dt.int32
U32 = mybir.dt.uint32
U16 = mybir.dt.uint16
U8 = mybir.dt.uint8
FP8X4 = mybir.dt.float8_e4m3fn_x4
FP4X4 = mybir.dt.float4_e2m1fn_x4
ALU = mybir.AluOpType
ACT = mybir.ActivationFunctionType

PART = 128
PACK = 4
PASS = PART * PACK
BANK = 512
QUADS = 4
QUAD = PART // QUADS
SCALE_ROWS = 4
LIST_ROWS = 16
LINE = 4
SCALAR_SHARE = 48


def tile_list_slotting_effort_scores_kernel(
    tc, tab_words, tab_scales, tab2_words, tab2_scales, offs, offs2, pos1, offs3, offs4,
    w1, w2_words, w2_scales, rate, w3, w4_words, w4_scales, b, wg1, wg2, page1, out,
):
    nc = tc.nc
    k_passes = K // PASS
    groups = H // PASS
    n_tiles = N // PART
    chunks = S // BANK

    with ExitStack() as ctx:
        keep = ctx.enter_context(tc.tile_pool(name="keep", bufs=1))
        raw_pool = ctx.enter_context(tc.tile_pool(name="raw", bufs=3))
        ring = ctx.enter_context(tc.tile_pool(name="ring", bufs=2))
        z_pool = ctx.enter_context(tc.tile_pool(name="zq", bufs=2 * groups))
        psum_h1 = ctx.enter_context(tc.psum_pool(name="psum_h1", bufs=4))
        psum_rest = ctx.enter_context(tc.psum_pool(name="psum_rest", bufs=4))

        def kept(shape, dtype, name):
            return keep.tile(shape, dtype, name=name, align_bytes=64)

        def load_list(src, name):
            tile = kept([PART, src.shape[1]], U16, name)
            nc.sync.dma_start(tile[:], src)
            return tile

        def load_words(src, name):
            tile = kept([PART, src.shape[1]], I32, name)
            nc.sync.dma_start(out=tile[:], in_=src.rearrange("p t i -> p (t i)").bitcast(I32))
            return tile

        def load_scale_rows(tile, src):
            rows = SCALE_ROWS * src.shape[0]
            for quad in range(QUADS):
                nc.sync.dma_start(
                    out=tile[QUAD * quad : QUAD * quad + rows, :].bitcast(I32),
                    in_=src[:, SCALE_ROWS * quad : SCALE_ROWS * (quad + 1), :].bitcast(I32),
                )

        def load_raw(src, name):
            tile = raw_pool.tile([PART, PACK, src.shape[1]], F32, name=name, tag="raw", align_bytes=64)
            nc.sync.dma_start(out=tile[:], in_=src.rearrange("(p j) c -> p j c", j=PACK))
            return tile

        def quantize(grouped, codes, scales):
            nc.vector.quantize_mx(
                out=codes[:].bitcast(FP8X4), scales=scales[:], in_=grouped[:].rearrange("p c j -> p (c j)")
            )

        def by_lines(planes):
            return planes.rearrange("p t (c i) -> p c t i", i=LINE)

        def by_lines_interleaved(grouped):
            return grouped.rearrange("p (c i) t -> p c t i", i=LINE)

        tab_sc = kept([PART, T], U8, "tab_sc")
        tab2_sc = kept([PART, T], U8, "tab2_sc")
        w2_sc_raw = kept([PART, H], U8, "w2_sc_raw")
        w4_sc = kept([PART, groups, N], U8, "w4_sc")
        nc.vector.memset(tab_sc[:].bitcast(I32), 0)
        nc.gpsimd.memset(tab2_sc[:].bitcast(I32), 0)
        nc.gpsimd.memset(w2_sc_raw[:].bitcast(I32), 0)
        nc.gpsimd.memset(w4_sc[:].bitcast(I32), 0)
        one = kept([PART, 1], F32, "one")
        half_pi = kept([PART, 1], F32, "half_pi")
        nc.gpsimd.memset(one[:], 1.0)
        nc.gpsimd.tensor_scalar(half_pi[:], one[:], math.pi / 2, 0.0, ALU.mult, ALU.add)
        warm = kept([PART, 1], F32, "warm")
        nc.scalar.activation(out=warm[:], in_=one[:], func=ACT.Sin)

        w1_raw = {}
        idx = load_list(offs, "idx")
        tab_w = [load_words(tab_words[0], "tab_w0")]
        load_scale_rows(tab_sc, tab_scales)
        tab_w.append(load_words(tab_words[1], "tab_w1"))
        for a in range(k_passes):
            w1_raw[a, 0] = load_raw(w1[a * PASS : (a + 1) * PASS, 0:PASS], "w1_raw%d0" % a)
        load_scale_rows(tab2_sc, tab2_scales)
        idx2 = load_list(offs2, "idx2")
        w2_raw = load_words(w2_words[0], "w2_raw")
        tab2_w = load_words(tab2_words[0], "tab2_w")
        p1 = load_list(pos1, "p1")
        load_scale_rows(w2_sc_raw, w2_scales)

        v_w = [kept([PART, S], U32, "v_w%d" % a) for a in range(k_passes)]
        v_sc = kept([PART, S], U8, "v_sc")
        nc.vector.tensor_copy(v_w[0][:], tab_w[0][:].bitcast(U32).indirect(idx[:]))
        nc.vector.tensor_copy(v_sc[:], tab_sc[:].indirect(idx[:]))
        nc.vector.tensor_copy(v_w[1][:], tab_w[1][:].bitcast(U32).indirect(idx[:]))

        w1_codes = {}
        w1_sc = {}
        w1_grouped = {}

        def quantize_w1(a, g):
            grouped = ring.tile([PART, PASS, PACK], BF16, name="w_grouped", tag="w_grouped", align_bytes=64)
            dst = grouped[:].rearrange("p (t m) j -> p m j t", t=PACK)
            src = w1_raw[a, g][:].rearrange("p j (m t) -> p m j t", t=PACK)
            if a < k_passes - 1:
                nc.scalar.copy(out=dst, in_=src)
            else:
                nc.scalar.copy(out=dst[:, :SCALAR_SHARE], in_=src[:, :SCALAR_SHARE])
                nc.vector.tensor_copy(out=dst[:, SCALAR_SHARE:], in_=src[:, SCALAR_SHARE:])
            w1_grouped[a, g] = grouped
            w1_codes[a, g] = kept([PART, PASS], U32, "w1_codes%d%d" % (a, g))
            w1_sc[a, g] = kept([PART, PASS], U8, "w1_sc%d%d" % (a, g))
            quantize(grouped, w1_codes[a, g], w1_sc[a, g])

        for a in range(k_passes):
            quantize_w1(a, 0)

        v2_w = kept([PART, S2], U32, "v2_w")
        v2_sc = kept([PART, S2], U8, "v2_sc")
        nc.vector.tensor_copy(v2_w[:], tab2_w[:].bitcast(U32).indirect(idx2[:]))
        nc.vector.tensor_copy(v2_sc[:], tab2_sc[:].indirect(idx2[:]))

        w2_codes = kept([PART, H], U32, "w2_codes")
        w2_sc = kept([PART, H], U8, "w2_sc")
        nc.vector.tensor_copy(
            out=w2_sc[:].rearrange("p (g t m) -> p g m t", g=groups, t=PACK),
            in_=w2_sc_raw[:].rearrange("p (g m t) -> p g m t", g=groups, t=PACK),
        )
        nc.scalar.copy(
            out=w2_codes[:].rearrange("p (g t m) -> p g m t", g=groups, t=PACK),
            in_=w2_raw[:].bitcast(U32).rearrange("p (g m t) -> p g m t", g=groups, t=PACK),
        )

        for a in range(k_passes):
            w1_raw[a, 1] = load_raw(w1[a * PASS : (a + 1) * PASS, PASS : 2 * PASS], "w1_raw%d1" % a)
        rate_sb = kept([PART, groups, PACK], F32, "rate_sb")
        nc.sync.dma_start(out=rate_sb[:], in_=rate.rearrange("(g p t) -> p g t", p=PART, t=PACK))
        w3_raw = [load_raw(w3[g * PASS : (g + 1) * PASS, :], "w3_raw%d" % g) for g in range(groups)]
        w4_w = kept([PART, groups, 2 * N], U8, "w4_w")
        nc.sync.dma_start(out=w4_w[:].bitcast(I32), in_=w4_words.rearrange("a p c -> p a c").bitcast(I32))
        for quad in range(QUADS):
            rows = w4_scales[:, SCALE_ROWS * quad : SCALE_ROWS * (quad + 1), :]
            nc.sync.dma_start(
                out=w4_sc[QUAD * quad : QUAD * quad + SCALE_ROWS, :, :].bitcast(I32),
                in_=rows.rearrange("a r c -> r a c").bitcast(I32),
            )
        wg2_sb = kept([PART, S2], F32, "wg2_sb")
        nc.sync.dma_start(out=wg2_sb[:], in_=wg2)
        idx4 = load_list(offs4, "idx4")
        b_sb = kept([PART, n_tiles], F32, "b_sb")
        with nc.allow_non_contiguous_dma(reason="one bias value a partition"):
            nc.sync.dma_start(out=b_sb[:], in_=b.rearrange("(i p) -> p i", p=PART))
        pages = []
        for i in range(n_tiles):
            page = kept([PART, T2], F32, "page%d" % i)
            nc.sync.dma_start(out=page[:], in_=page1[i * PART : (i + 1) * PART, :])
            pages.append(page)
        wg1_sb = kept([PART, S], F32, "wg1_sb")
        nc.sync.dma_start(out=wg1_sb[:], in_=wg1)
        idx3 = load_list(offs3, "idx3")

        h1 = [kept([PART, PACK, S], F32, "h1_%d" % g) for g in range(groups)]
        z2_codes = []
        z2_sc = []
        for g in range(groups):
            picked = ring.tile([PART, PACK, S2], F32, name="picked", tag="picked", align_bytes=64)
            for t in range(PACK):
                places = slice(t * PART, (t + 1) * PART)
                for c in range(chunks):
                    js = slice(c * BANK, (c + 1) * BANK)
                    acc = psum_h1.tile([PART, BANK], F32, name="acc_h1", tag="acc_h1")
                    for a in range(k_passes):
                        nc.tensor.matmul_mx(
                            out=acc[:],
                            lhsT=w1_codes[a, g][:, places].bitcast(FP8X4),
                            lhsT_scale=w1_sc[a, g][:, places],
                            rhs=v_w[a][:, js].bitcast(FP8X4),
                            rhs_scale=v_sc[SCALE_ROWS * a : PART, js],
                            start=(a == 0),
                            stop=(a == k_passes - 1),
                        )
                    nc.scalar.copy(out=h1[g][:, t, js], in_=acc[:])
                nc.vector.tensor_copy(picked[:, t, :], h1[g][:, t, :].indirect(p1[:]))

            if g + 1 < groups:
                for a in range(k_passes):
                    quantize_w1(a, g + 1)
                z2 = w1_grouped[0, g + 1]
            else:
                z2 = ring.tile([PART, S2, PACK], BF16, name="z2", tag="z", align_bytes=64)
            for j0 in range(0, S2, PART):
                js = slice(j0, j0 + PART)
                acc = psum_rest.tile([PART, PACK, PART], F32, name="acc_h2", tag="acc")
                for t in range(PACK):
                    places = slice(g * PASS + t * PART, g * PASS + (t + 1) * PART)
                    nc.tensor.matmul_mx(
                        out=acc[:, t, :],
                        lhsT=w2_codes[:, places].bitcast(FP8X4),
                        lhsT_scale=w2_sc[:, places],
                        rhs=v2_w[:, js].bitcast(FP8X4),
                        rhs_scale=v2_sc[:, js],
                        start=True,
                        stop=True,
                    )
                nc.vector.tensor_tensor(
                    out=by_lines_interleaved(z2[:, js, :]),
                    in0=by_lines(picked[:, :, js]),
                    in1=by_lines(acc[:]),
                    op=ALU.max,
                )
            codes = z_pool.tile([PART, S2], U32, name="z2_codes", tag="z_codes", align_bytes=64)
            scales = z_pool.tile([PART, S2], U8, name="z2_sc", tag="z_sc", align_bytes=64)
            quantize(z2, codes, scales)
            z2_codes.append(codes)
            z2_sc.append(scales)

        y2_acc = []
        for i in range(n_tiles):
            acc = psum_rest.tile([PART, BANK], F32, name="acc_y2", tag="acc")
            for g in range(groups):
                nc.tensor.matmul_mx(
                    out=acc[:],
                    lhsT=w4_w[:, g, 2 * i * PART : 2 * (i + 1) * PART].bitcast(FP4X4),
                    lhsT_scale=w4_sc[:, g, i * PART : (i + 1) * PART],
                    rhs=z2_codes[g][:].bitcast(FP8X4),
                    rhs_scale=z2_sc[g][:],
                    start=(g == 0),
                    stop=(g == groups - 1),
                )
            y2_acc.append(acc)

        cosines = {}
        z1_codes = {}
        z1_sc = {}

        def make_z1(c):
            js = slice(c * BANK, (c + 1) * BANK)
            for g in range(groups):
                cos = kept([PART, PACK, BANK], F32, "cos%d%d" % (c, g))
                cosines[c, g] = cos
                for t in range(PACK):
                    nc.scalar.activation(
                        out=cos[:, t, :], in_=h1[g][:, t, js], func=ACT.Abs, scale=rate_sb[:, g, t : t + 1]
                    )
                for t in range(PACK):
                    nc.scalar.activation(
                        out=cos[:, t, :], in_=cos[:, t, :], func=ACT.Sin, scale=-1.0, bias=half_pi[:]
                    )
                z1 = ring.tile([PART, BANK, PACK], BF16, name="z1", tag="z", align_bytes=64)
                nc.vector.tensor_tensor(
                    out=by_lines_interleaved(z1[:]),
                    in0=by_lines(cos[:]),
                    in1=by_lines(h1[g][:, :, js]),
                    op=ALU.mult,
                )
                z1_codes[c, g] = z_pool.tile([PART, BANK], U32, name="z1_codes", tag="z_codes", align_bytes=64)
                z1_sc[c, g] = z_pool.tile([PART, BANK], U8, name="z1_sc", tag="z_sc", align_bytes=64)
                quantize(z1, z1_codes[c, g], z1_sc[c, g])

        make_z1(0)

        w3_codes = []
        w3_sc = []
        for g in range(groups):
            grouped = ring.tile([PART, N, PACK], BF16, name="w3_grouped", tag="w_grouped", align_bytes=64)
            nc.scalar.copy(out=by_lines_interleaved(grouped[:]), in_=by_lines(w3_raw[g][:]))
            w3_codes.append(kept([PART, N], U32, "w3_codes%d" % g))
            w3_sc.append(kept([PART, N], U8, "w3_sc%d" % g))
            quantize(grouped, w3_codes[g], w3_sc[g])

        staged = cosines[0, groups - 1]
        for i in range(n_tiles):
            nc.scalar.activation(
                out=staged[:, i, :], in_=y2_acc[i][:], func=ACT.Identity, bias=b_sb[:, i : i + 1]
            )
            nc.vector.tensor_tensor(
                out=pages[i][:].indirect(idx4[:]), in0=staged[:, i, :], in1=wg2_sb[:], op=ALU.mult
            )

        make_z1(1)

        staging = [[cosines[1, 0]] * (n_tiles - 1) + [cosines[1, groups - 1]], [cosines[0, 0]] * n_tiles]
        for c in range(chunks):
            js = slice(c * BANK, (c + 1) * BANK)
            entries = idx3[:, c * BANK // LIST_ROWS : (c + 1) * BANK // LIST_ROWS]
            for i in range(n_tiles):
                ns = slice(i * PART, (i + 1) * PART)
                acc = psum_rest.tile([PART, BANK], F32, name="acc_y1", tag="acc")
                for g in range(groups):
                    nc.tensor.matmul_mx(
                        out=acc[:],
                        lhsT=w3_codes[g][:, ns].bitcast(FP8X4),
                        lhsT_scale=w3_sc[g][:, ns],
                        rhs=z1_codes[c, g][:].bitcast(FP8X4),
                        rhs_scale=z1_sc[c, g][:],
                        start=(g == 0),
                        stop=(g == groups - 1),
                    )
                staged = staging[c][i]
                nc.scalar.copy(out=staged[:, i, :], in_=acc[:])
                nc.vector.tensor_tensor(
                    out=pages[i][:].indirect(entries), in0=staged[:, i, :], in1=wg1_sb[:, js], op=ALU.mult
                )
                if c == chunks - 1:
                    nc.sync.dma_start(out=out[ns, :], in_=pages[i][:])
